import numpy as np
import ml_dtypes


def mxq(x, axis, fmt="e4m3"):
    dtype, down = {"e4m3": (ml_dtypes.float8_e4m3fn, 7), "e5m2": (ml_dtypes.float8_e5m2, 14)}[fmt]
    v = np.moveaxis(np.asarray(x, np.float32).astype(ml_dtypes.bfloat16).astype(np.float64), axis, -1)
    blocks = v.reshape(v.shape[:-1] + (-1, 32))
    amax = np.abs(blocks).max(-1, keepdims=True)
    byte = np.maximum(np.where(amax > 0, np.frexp(amax)[1] - 1 + 127, 0) - down, 1)
    scale = np.exp2(byte - 127.0)
    codes = (blocks / scale).astype(np.float32).astype(dtype).astype(np.float64)
    return np.moveaxis((codes * scale).reshape(v.shape), -1, axis)


WIDE = False


def mx_kscale(k):
    if not WIDE:
        return np.ones(k)
    levels = np.array([10, -10, 5, -5, 0])
    if k % 512:
        return np.exp2(np.random.permutation(np.resize(levels, k // 32))).repeat(32)
    a = np.empty((k // 512, 16))
    for p in range(k // 512):
        a[p, :8] = np.random.permutation(np.resize(levels, 8))
        for g in range(8):
            far = levels[np.abs(levels - a[p, g]) >= 10]
            a[p, g + 8] = far[np.random.randint(len(far))]
    return np.exp2(a.ravel()).repeat(32)


def f64(x):
    return np.asarray(x).astype(np.float64)


def striped(idx):
    return np.tile(np.asarray(idx).reshape(-1, 16).T, (8, 1)).astype(np.uint16)


def unstriped(offs):
    return offs[:16].T.reshape(-1).astype(np.int64)


E2M1 = np.array([0.0, 0.5, 1.0, 1.5, 2.0, 3.0, 4.0, 6.0, -0.0, -0.5, -1.0, -1.5, -2.0, -3.0, -4.0, -6.0])


def pack_weight(w, fmt):
    k, n = w.shape
    w = f64(np.asarray(w, np.float32).astype(ml_dtypes.bfloat16)).reshape(k // 32, 32, n)
    amax = np.abs(w).max(1)
    if fmt == "e4m3":
        byte = np.frexp(amax)[1] - 1 + 127 - 7
    else:
        mant, ex = np.frexp(amax / 6.0)
        byte = np.where(mant > 0.5, ex, ex - 1) + 127
    byte = np.clip(np.where(amax > 0, byte, 1), 1, 254)
    scaled = (w * np.exp2(127.0 - byte)[:, None, :]).reshape(k, n).astype(np.float32)
    by_word = np.ascontiguousarray(scaled.reshape(k // 512, 128, 4, n).transpose(0, 1, 3, 2))
    if fmt == "e4m3":
        words = by_word.astype(ml_dtypes.float8_e4m3fn).view(np.uint8)
    else:
        c = by_word.astype(ml_dtypes.float4_e2m1fn).view(np.uint8) & 0xF
        words = (c[..., 0::2] | (c[..., 1::2] << 4)).reshape(k // 512, 128, 2 * n)
    return np.ascontiguousarray(words), np.ascontiguousarray(byte.astype(np.uint8).reshape(k // 512, 16, n))


def unpack_weight(words, scales, fmt):
    g, _, n = scales.shape
    words = np.ascontiguousarray(words).reshape(g, 128, n, -1)
    if fmt == "e4m3":
        vals = words.view(ml_dtypes.float8_e4m3fn).astype(np.float64)
    else:
        nib = np.empty((g, 128, n, 4), np.uint8)
        nib[..., 0::2] = words & 0xF
        nib[..., 1::2] = words >> 4
        vals = E2M1[nib]
    vals = vals * np.repeat(np.exp2(scales.astype(np.float64) - 127.0), 8, axis=1)[..., None]
    return vals.transpose(0, 1, 3, 2).reshape(g * 512, n)


def softplus(v):
    return np.log(1.0 + np.exp(v))


def sigmoid(v):
    return 1.0 / (1.0 + np.exp(-v))


D, K, R, T, I, Q, U = 512, 512, 512, 2048, 512, 128, 1024


def setup_inputs():
    n = np.random.standard_normal
    idx2 = np.random.permutation(U)[:I]
    idx = np.random.permutation(T)[:I]
    fd = mx_kscale(D)
    fk = mx_kscale(K)
    fi = mx_kscale(I)
    keysp = pack_weight(n((D, T)) / fd[:, None], "e4m3")
    tabp = pack_weight(n((K, T)) / fk[:, None], "e4m3")
    return {
        "query": (n((D, Q)) * 0.9 / np.sqrt(D) * fd[:, None]).astype(np.float32),
        "keys_words": keysp[0],
        "keys_scales": keysp[1],
        "th": (np.random.uniform(-0.3, 0.6, (Q, 1))).astype(np.float32),
        "reserve": (np.random.uniform(50.0, 200.0, (Q, 1))).astype(np.float32),
        "tab_words": tabp[0],
        "tab_scales": tabp[1],
        "w1": (n((K, R)) * 1 / np.sqrt(K) * fk[:, None]).astype(np.float32),
        "gtab": (n((R, U))).astype(np.float32),
        "os": (np.random.uniform(4.0, 16.0, (1, I)) * fi).astype(np.float32),
        "vs": (np.random.uniform(0.5, 2.0, (1, I)) / fi).astype(np.float32),
        "offs2": striped(idx2),
        "offs": striped(idx),
    }


def reference(query, keys_words, keys_scales, th, reserve, tab_words, tab_scales, w1, gtab, os, vs, offs2, offs):
    idx2 = unstriped(offs2)
    idx = unstriped(offs)
    keysu = unpack_weight(keys_words, keys_scales, "e4m3")
    tabu = unpack_weight(tab_words, tab_scales, "e4m3")
    queryq = mxq(f64(query), 0, "e4m3")
    keysidxg = keysu[:, idx]
    a = queryq.T @ keysidxg
    p = softplus(a - f64(th))
    z = np.sum(p, axis=1, keepdims=True) + f64(reserve)
    w = p / z
    w1q = mxq(f64(w1), 0, "e4m3")
    tabidxg = tabu[:, idx]
    zh = w1q.T @ tabidxg
    hg = sigmoid(f64(gtab)[:, idx2])
    hv = zh * hg
    wo1 = w * f64(os)
    wt1 = wo1.T
    hw = hv * f64(vs)
    ht1 = hw.T
    wt1q = mxq(wt1, 0, "e4m3")
    ht1q = mxq(ht1, 0, "e4m3")
    o = wt1q.T @ ht1q
    return o

@@ -1,0 +1,202 @@
+from contextlib import ExitStack
+
+import concourse.mybir as mybir
+from concourse.masks import make_identity
+
+F32 = mybir.dt.float32
+BF16 = mybir.dt.bfloat16
+I32 = mybir.dt.int32
+U32 = mybir.dt.uint32
+U16 = mybir.dt.uint16
+U8 = mybir.dt.uint8
+FP8X4 = mybir.dt.float8_e4m3fn_x4
+ALU = mybir.AluOpType
+ACT = mybir.ActivationFunctionType
+
+P = 128
+PACK = 4
+D, K, R, T, I, Q, U = 512, 512, 512, 2048, 512, 128, 1024
+BLOCKS = R // P
+HALF = R // 2
+EXP_CAP = 2.0**40
+
+FLOPS = 2 * (Q * I * D + R * I * K + Q * R * I)
+
+
+def tile_attend_lrgated_capped_kernel(
+    tc, query, keys_words, keys_scales, th, reserve, tab_words, tab_scales, w1, gtab, slot_factor, value_scale, offs2, offs, out
+):
+    nc = tc.nc
+    with ExitStack() as ctx:
+        sb = ctx.enter_context(tc.tile_pool(name="sb", bufs=1))
+        ps = ctx.enter_context(tc.psum_pool(name="ps", bufs=1))
+
+        def words_of(packed):
+            return packed[0].rearrange("p n t -> p (n t)").bitcast(I32)
+
+        def load_scale_rows(plane, rows):
+            for quad in range(4):
+                nc.scalar.dma_start(
+                    out=plane[32 * quad : 32 * quad + 4, :].bitcast(I32),
+                    in_=rows[0, 4 * quad : 4 * quad + 4, :].bitcast(I32),
+                )
+
+        def interleave(copy, dst, src):
+            copy(
+                out=dst.rearrange("p (c i t) -> p c t i", i=4, t=PACK),
+                in_=src.rearrange("p t (c i) -> p c t i", i=4),
+            )
+
+        def quantize(name, src, tag=""):
+            width = src.shape[1] // PACK
+            codes = sb.tile([P, width], U32, name=name + "_codes", tag=tag or name + "_codes", align_bytes=64)
+            scales = sb.tile([P, width], U8, name=name + "_scales", align_bytes=64)
+            nc.vector.quantize_mx(out=codes[:].bitcast(FP8X4), scales=scales[:], in_=src)
+            return codes, scales
+
+        def load_w1_half(h, tag):
+            raw = sb.tile([P, PACK, HALF], F32, name=f"w1_raw{h}", tag=tag, align_bytes=64)
+            rows = w1.rearrange("(p t) r -> p t r", t=PACK)
+            nc.sync.dma_start(out=raw[:], in_=rows[:, :, h * HALF : (h + 1) * HALF])
+            return raw
+
+        def load_gates(j, tag):
+            pool_j = sb.tile([P, U], F32, name=f"gate_pool{j}", tag=tag, align_bytes=64)
+            nc.sync.dma_start(out=pool_j[:], in_=gtab[j * P : (j + 1) * P, :])
+            return pool_j
+
+        key_plane = sb.tile([P, T], U8, tag="slot_c", align_bytes=64)
+        nc.vector.memset(key_plane[:].bitcast(I32), 0)
+        token_list = sb.tile([P, I // 16], U16)
+        nc.sync.dma_start(token_list[:], offs)
+        gate_list = sb.tile([P, I // 16], U16)
+        nc.sync.dma_start(gate_list[:], offs2)
+        q_raw = sb.tile([P, PACK, Q], F32, tag="slot_a", align_bytes=64)
+        nc.sync.dma_start(out=q_raw[:], in_=query.rearrange("(p t) q -> p t q", t=PACK))
+        key_pool = sb.tile([P, T], U32, tag="slot_d", align_bytes=64)
+        nc.sync.dma_start(out=key_pool[:].bitcast(I32), in_=words_of(keys_words))
+        load_scale_rows(key_plane, keys_scales)
+
+        th_col = sb.tile([P, 1], F32)
+        nc.gpsimd.dma_start(out=th_col[:], in_=th)
+        ident = sb.tile([P, P], F32)
+        make_identity(nc, ident[:])
+        os_cols = sb.tile([P, PACK], F32)
+        nc.gpsimd.dma_start(out=os_cols[:], in_=slot_factor.rearrange("o (s t) -> (o s) t", t=PACK))
+        reserve_col = sb.tile([P, 1], F32)
+        nc.gpsimd.dma_start(out=reserve_col[:], in_=reserve)
+        vs_cols = sb.tile([P, PACK], F32)
+        nc.gpsimd.dma_start(out=vs_cols[:], in_=value_scale.rearrange("o (s t) -> (o s) t", t=PACK))
+
+        q_bf = sb.tile([P, Q * PACK], BF16, tag="slot_b", align_bytes=64)
+        interleave(nc.scalar.copy, q_bf[:], q_raw[:])
+        neg_th = sb.tile([P, 1], F32)
+        nc.scalar.mul(neg_th[:], th_col[:], -1.0)
+        tab_pool = sb.tile([P, T], U32, tag="slot_a", align_bytes=64)
+        nc.sync.dma_start(out=tab_pool[:].bitcast(I32), in_=words_of(tab_words))
+        q_codes, q_scales = quantize("q", q_bf[:], "slot_f")
+        tab_plane = sb.tile([P, T], U8, tag="slot_b", align_bytes=64)
+        nc.vector.memset(tab_plane[:].bitcast(I32), 0)
+        load_scale_rows(tab_plane, tab_scales)
+        key_scales = sb.tile([P, I], U8, align_bytes=64)
+        nc.vector.tensor_copy(key_scales[:], key_plane[:].indirect(token_list[:]))
+        w1_raw = [load_w1_half(0, "slot_c")]
+        key_codes = sb.tile([P, I], U32, tag="slot_e", align_bytes=64)
+        nc.vector.tensor_copy(key_codes[:], key_pool[:].indirect(token_list[:]))
+        scores = ps.tile([P, I], F32, tag="score_bank")
+        nc.tensor.matmul_mx(
+            out=scores[:], lhsT=q_codes[:].bitcast(FP8X4), lhsT_scale=q_scales[:],
+            rhs=key_codes[:].bitcast(FP8X4), rhs_scale=key_scales[:], start=True, stop=True,
+        )
+        w1_raw.append(load_w1_half(1, "slot_e"))
+        gate_pool = [load_gates(0, "slot_f")]
+        os_rows = ps.tile([P, PACK, P], F32)
+        for t in range(PACK):
+            nc.tensor.transpose(os_rows[:, t, :], os_cols[:, t : t + 1].to_broadcast([P, P]), ident[:])
+
+        tab_scale_bytes = sb.tile([P, I], U8, tag="slot_d", align_bytes=64)
+        nc.vector.tensor_copy(tab_scale_bytes[:], tab_plane[:].indirect(token_list[:]))
+        gate_pool.append(load_gates(1, "slot_b"))
+
+        exps = sb.tile([P, I], F32, tag="slot_g", align_bytes=64)
+        nc.scalar.activation(exps[:], scores[:], ACT.Exp, bias=neg_th[:])
+        capped = sb.tile([P, I], F32)
+        nc.gpsimd.tensor_scalar(capped[:], exps[:], EXP_CAP, 0.0, ALU.min, ALU.max)
+        gate_pool.append(load_gates(2, "slot_g"))
+        logs = sb.tile([P, I], F32)
+        nc.scalar.activation(logs[:], capped[:], ACT.Ln, bias=1.0)
+
+        tab_codes = sb.tile([P, I], U32, align_bytes=64)
+        nc.vector.tensor_copy(tab_codes[:], tab_pool[:].indirect(token_list[:]))
+
+        gate_pool.append(load_gates(3, "slot_a"))
+        w1_q = []
+        for h in range(2):
+            w1_bf = sb.tile([P, HALF * PACK], BF16, name=f"w1_bf{h}", align_bytes=64)
+            interleave(nc.vector.tensor_copy, w1_bf[:], w1_raw[h][:])
+            w1_q.append(quantize(f"w1_{h}", w1_bf[:]))
+
+        soft = sb.tile([P, I], F32)
+        row_sum = sb.tile([P, 1], F32)
+        nc.vector.scalar_tensor_tensor(
+            soft[:], scores[:], th_col[:], logs[:], ALU.subtract, ALU.max, accum_out=row_sum[:]
+        )
+        z = sb.tile([P, 1], F32)
+        nc.vector.tensor_tensor(z[:], row_sum[:], reserve_col[:], ALU.add)
+        inv_z = sb.tile([P, 1], F32)
+        nc.vector.reciprocal(inv_z[:], z[:])
+        w_bf = sb.tile([P, I], BF16)
+        nc.vector.scalar_tensor_tensor(
+            w_bf[:].rearrange("p (s t) -> p s t", t=PACK),
+            soft[:].rearrange("p (s t) -> p s t", t=PACK),
+            inv_z[:],
+            os_rows[:].rearrange("p t s -> p s t"),
+            ALU.mult,
+            ALU.mult,
+        )
+        w_pairs = w_bf[:].bitcast(F32)
+        w_turned = ps.tile([P, 2, Q], F32, tag="score_bank")
+        for u in range(2):
+            nc.tensor.transpose(w_turned[:, u, :], w_pairs[:, u : I // 2 : 2], ident[:])
+        wt_bf = sb.tile([P, Q * PACK], BF16, align_bytes=64)
+        nc.scalar.copy(
+            out=wt_bf[:].bitcast(F32).rearrange("p (q u) -> p q u", u=2),
+            in_=w_turned[:].rearrange("p u q -> p q u"),
+        )
+        wt_codes, wt_scales = quantize("wt", wt_bf[:])
+
+        result = ps.tile([P, R], F32)
+        for j in range(BLOCKS):
+            h, cols = j // 2, slice((j % 2) * P, (j % 2 + 1) * P)
+            gate = sb.tile([P, I], F32, name=f"gate{j}")
+            nc.scalar.activation(gate[:], gate_pool[j][:].indirect(gate_list[:]), ACT.Sigmoid)
+            zh = ps.tile([P, I], F32, bufs=3)
+            nc.tensor.matmul_mx(
+                out=zh[:], lhsT=w1_q[h][0][:, cols].bitcast(FP8X4), lhsT_scale=w1_q[h][1][:, cols],
+                rhs=tab_codes[:].bitcast(FP8X4), rhs_scale=tab_scale_bytes[:], start=True, stop=True,
+            )
+            hv = sb.tile([P, PACK, P], F32, name=f"hv{j}")
+            nc.vector.tensor_tensor(
+                hv[:].rearrange("p t (c i) -> p c t i", i=4),
+                zh[:].rearrange("p (c i t) -> p c t i", i=4, t=PACK),
+                gate[:].rearrange("p (c i t) -> p c t i", i=4, t=PACK),
+                ALU.mult,
+            )
+            h_turned = ps.tile([P, PACK, P], F32, bufs=2)
+            for t in range(PACK):
+                nc.tensor.transpose(h_turned[:, t, :], hv[:, t, :], ident[:])
+            ht_bf = sb.tile([P, P * PACK], BF16, name=f"ht_bf{j}", align_bytes=64)
+            nc.vector.tensor_tensor(
+                ht_bf[:].rearrange("p (r t) -> p r t", t=PACK),
+                h_turned[:].rearrange("p t r -> p r t"),
+                vs_cols[:].unsqueeze(1).to_broadcast([P, P, PACK]),
+                ALU.mult,
+            )
+            ht_codes, ht_scales = quantize(f"ht{j}", ht_bf[:])
+            nc.tensor.matmul_mx(
+                out=result[:, j * P : (j + 1) * P], lhsT=wt_codes[:].bitcast(FP8X4), lhsT_scale=wt_scales[:],
+                rhs=ht_codes[:].bitcast(FP8X4), rhs_scale=ht_scales[:], start=True, stop=True,
+            )
+            staged = sb.tile([P, P], F32, name=f"staged{j}")
+            nc.scalar.copy(staged[:], result[:, j * P : (j + 1) * P])
+            nc.sync.dma_start(out=out[:, j * P : (j + 1) * P], in_=staged[:])

@@ -15,10 +15,17 @@ ACT = mybir.ActivationFunctionType
 
 P = 128
 PACK = 4
+QUADRANT = 32
+SCALE_ROWS = 4
+LIST_ROWS = 16
+RUN = 4
+MX_ALIGN = 64
 D, K, R, T, I, Q, U = 512, 512, 512, 2048, 512, 128, 1024
 BLOCKS = R // P
 HALF = R // 2
-EXP_CAP = 2.0**40
+PRODUCT_BANKS = BLOCKS
+TURN_BANKS = 2
+SIGMOID_FLOOR = 2.0**-24
 
 FLOPS = 2 * (Q * I * D + R * I * K + Q * R * I)
 
@@ -31,125 +38,128 @@ def tile_attend_lrgated_capped_kernel(
         sb = ctx.enter_context(tc.tile_pool(name="sb", bufs=1))
         ps = ctx.enter_context(tc.psum_pool(name="ps", bufs=1))
 
+
         def words_of(packed):
             return packed[0].rearrange("p n t -> p (n t)").bitcast(I32)
 
         def load_scale_rows(plane, rows):
-            for quad in range(4):
-                nc.scalar.dma_start(
-                    out=plane[32 * quad : 32 * quad + 4, :].bitcast(I32),
-                    in_=rows[0, 4 * quad : 4 * quad + 4, :].bitcast(I32),
+            for g in range(P // QUADRANT):
+                nc.sync.dma_start(
+                    out=plane[QUADRANT * g : QUADRANT * g + SCALE_ROWS, :].bitcast(I32),
+                    in_=rows[0, SCALE_ROWS * g : SCALE_ROWS * (g + 1), :].bitcast(I32),
                 )
 
-        def interleave(copy, dst, src):
-            copy(
-                out=dst.rearrange("p (c i t) -> p c t i", i=4, t=PACK),
-                in_=src.rearrange("p t (c i) -> p c t i", i=4),
-            )
-
-        def quantize(name, src, tag=""):
-            width = src.shape[1] // PACK
-            codes = sb.tile([P, width], U32, name=name + "_codes", tag=tag or name + "_codes", align_bytes=64)
-            scales = sb.tile([P, width], U8, name=name + "_scales", align_bytes=64)
-            nc.vector.quantize_mx(out=codes[:].bitcast(FP8X4), scales=scales[:], in_=src)
-            return codes, scales
-
-        def load_w1_half(h, tag):
-            raw = sb.tile([P, PACK, HALF], F32, name=f"w1_raw{h}", tag=tag, align_bytes=64)
+        def load_w1_half(h):
+            raw = sb.tile([P, PACK, HALF], F32, name=f"w1_raw{h}")
             rows = w1.rearrange("(p t) r -> p t r", t=PACK)
             nc.sync.dma_start(out=raw[:], in_=rows[:, :, h * HALF : (h + 1) * HALF])
             return raw
 
-        def load_gates(j, tag):
-            pool_j = sb.tile([P, U], F32, name=f"gate_pool{j}", tag=tag, align_bytes=64)
+        def load_gates(j):
+            pool_j = sb.tile([P, U], F32, name=f"gate_pool{j}", tag=f"gate_pool_slot{j}", align_bytes=MX_ALIGN)
             nc.sync.dma_start(out=pool_j[:], in_=gtab[j * P : (j + 1) * P, :])
             return pool_j
 
-        key_plane = sb.tile([P, T], U8, tag="slot_c", align_bytes=64)
-        nc.vector.memset(key_plane[:].bitcast(I32), 0)
-        token_list = sb.tile([P, I // 16], U16)
-        nc.sync.dma_start(token_list[:], offs)
-        gate_list = sb.tile([P, I // 16], U16)
-        nc.sync.dma_start(gate_list[:], offs2)
-        q_raw = sb.tile([P, PACK, Q], F32, tag="slot_a", align_bytes=64)
-        nc.sync.dma_start(out=q_raw[:], in_=query.rearrange("(p t) q -> p t q", t=PACK))
-        key_pool = sb.tile([P, T], U32, tag="slot_d", align_bytes=64)
-        nc.sync.dma_start(out=key_pool[:].bitcast(I32), in_=words_of(keys_words))
-        load_scale_rows(key_plane, keys_scales)
+        def as_words(grouped):
+            return grouped.rearrange("p (c i t) -> p c t i", i=RUN, t=PACK)
 
-        th_col = sb.tile([P, 1], F32)
-        nc.gpsimd.dma_start(out=th_col[:], in_=th)
+        def as_places(planar):
+            return planar.rearrange("p t (c i) -> p c t i", i=RUN)
+
+        def quantize(name, src):
+            width = src.shape[1] // PACK
+            codes = sb.tile([P, width], U32, name=name + "_codes", align_bytes=MX_ALIGN)
+            scales = sb.tile([P, width], U8, name=name + "_scales", align_bytes=MX_ALIGN)
+            nc.vector.quantize_mx(out=codes[:].bitcast(FP8X4), scales=scales[:], in_=src)
+            return codes, scales
+
+        def gate_of(j):
+            gate = sb.tile([P, I], F32, name=f"gate{j}", tag=f"gate_slot{j}", align_bytes=MX_ALIGN)
+            nc.scalar.activation(gate[:], gate_pool[j][:].indirect(gate_list[:]), ACT.Sigmoid)
+            return gate
+
+        key_plane = sb.tile([P, T], U8)
+        nc.gpsimd.memset(key_plane[:, : T // 2].bitcast(I32), 0)
+        nc.vector.memset(key_plane[:, T // 2 :].bitcast(I32), 0)
+        tab_plane = sb.tile([P, T], U8)
+        nc.vector.memset(tab_plane[:].bitcast(I32), 0)
         ident = sb.tile([P, P], F32)
         make_identity(nc, ident[:])
-        os_cols = sb.tile([P, PACK], F32)
-        nc.gpsimd.dma_start(out=os_cols[:], in_=slot_factor.rearrange("o (s t) -> (o s) t", t=PACK))
-        reserve_col = sb.tile([P, 1], F32)
-        nc.gpsimd.dma_start(out=reserve_col[:], in_=reserve)
-        vs_cols = sb.tile([P, PACK], F32)
-        nc.gpsimd.dma_start(out=vs_cols[:], in_=value_scale.rearrange("o (s t) -> (o s) t", t=PACK))
 
-        q_bf = sb.tile([P, Q * PACK], BF16, tag="slot_b", align_bytes=64)
-        interleave(nc.scalar.copy, q_bf[:], q_raw[:])
-        neg_th = sb.tile([P, 1], F32)
-        nc.scalar.mul(neg_th[:], th_col[:], -1.0)
-        tab_pool = sb.tile([P, T], U32, tag="slot_a", align_bytes=64)
-        nc.sync.dma_start(out=tab_pool[:].bitcast(I32), in_=words_of(tab_words))
-        q_codes, q_scales = quantize("q", q_bf[:], "slot_f")
-        tab_plane = sb.tile([P, T], U8, tag="slot_b", align_bytes=64)
-        nc.vector.memset(tab_plane[:].bitcast(I32), 0)
+        token_list = sb.tile([P, I // LIST_ROWS], U16)
+        nc.sync.dma_start(token_list[:], offs)
+        q_raw = sb.tile([P, PACK, Q], F32)
+        nc.sync.dma_start(out=q_raw[:], in_=query.rearrange("(p t) q -> p t q", t=PACK))
+        gate_list = sb.tile([P, I // LIST_ROWS], U16)
+        nc.sync.dma_start(gate_list[:], offs2)
+        load_scale_rows(key_plane, keys_scales)
+        key_pool = sb.tile([P, T], U32, tag="key_pool_slot", align_bytes=MX_ALIGN)
+        nc.sync.dma_start(out=key_pool[:].bitcast(I32), in_=words_of(keys_words))
         load_scale_rows(tab_plane, tab_scales)
-        key_scales = sb.tile([P, I], U8, align_bytes=64)
+        th_col = sb.tile([P, 1], F32)
+        nc.sync.dma_start(out=th_col[:], in_=th)
+        gate_pool = [load_gates(0)]
+        w1_raw = [load_w1_half(0)]
+        tab_pool = sb.tile([P, T], U32, tag="tab_pool_slot")
+        nc.sync.dma_start(out=tab_pool[:].bitcast(I32), in_=words_of(tab_words))
+        w1_raw.append(load_w1_half(1))
+        os_cols = sb.tile([P, PACK], F32)
+        nc.sync.dma_start(out=os_cols[:], in_=slot_factor.rearrange("o (s t) -> (o s) t", t=PACK))
+        reserve_col = sb.tile([P, 1], F32)
+        nc.sync.dma_start(out=reserve_col[:], in_=reserve)
+        vs_cols = sb.tile([P, PACK], F32)
+        nc.sync.dma_start(out=vs_cols[:], in_=value_scale.rearrange("o (s t) -> (o s) t", t=PACK))
+        gate_pool.extend([load_gates(j) for j in range(1, BLOCKS)])
+
+        q_bf = sb.tile([P, Q * PACK], BF16, align_bytes=MX_ALIGN)
+        nc.vector.tensor_scalar(as_words(q_bf[:]), as_places(q_raw[:]), -1.0, None, ALU.mult)
+        key_scales = sb.tile([P, I], U8, align_bytes=MX_ALIGN)
         nc.vector.tensor_copy(key_scales[:], key_plane[:].indirect(token_list[:]))
-        w1_raw = [load_w1_half(0, "slot_c")]
-        key_codes = sb.tile([P, I], U32, tag="slot_e", align_bytes=64)
+        q_codes, q_scales = quantize("q", q_bf[:])
+        key_codes = sb.tile([P, I], U32, align_bytes=MX_ALIGN)
         nc.vector.tensor_copy(key_codes[:], key_pool[:].indirect(token_list[:]))
-        scores = ps.tile([P, I], F32, tag="score_bank")
+        neg_scores = ps.tile([P, I], F32, tag="score_bank")
         nc.tensor.matmul_mx(
-            out=scores[:], lhsT=q_codes[:].bitcast(FP8X4), lhsT_scale=q_scales[:],
+            out=neg_scores[:], lhsT=q_codes[:].bitcast(FP8X4), lhsT_scale=q_scales[:],
             rhs=key_codes[:].bitcast(FP8X4), rhs_scale=key_scales[:], start=True, stop=True,
         )
-        w1_raw.append(load_w1_half(1, "slot_e"))
-        gate_pool = [load_gates(0, "slot_f")]
         os_rows = ps.tile([P, PACK, P], F32)
         for t in range(PACK):
             nc.tensor.transpose(os_rows[:, t, :], os_cols[:, t : t + 1].to_broadcast([P, P]), ident[:])
 
-        tab_scale_bytes = sb.tile([P, I], U8, tag="slot_d", align_bytes=64)
+        tab_scale_bytes = sb.tile([P, I], U8, tag="key_pool_slot", align_bytes=MX_ALIGN)
         nc.vector.tensor_copy(tab_scale_bytes[:], tab_plane[:].indirect(token_list[:]))
-        gate_pool.append(load_gates(1, "slot_b"))
+        w1_bf = [sb.tile([P, HALF * PACK], BF16, name=f"w1_bf{h}", align_bytes=MX_ALIGN) for h in range(2)]
+        nc.vector.tensor_copy(out=as_words(w1_bf[0][:]), in_=as_places(w1_raw[0][:]))
+        w1_q = [quantize("w1_0", w1_bf[0][:])]
 
-        exps = sb.tile([P, I], F32, tag="slot_g", align_bytes=64)
-        nc.scalar.activation(exps[:], scores[:], ACT.Exp, bias=neg_th[:])
-        capped = sb.tile([P, I], F32)
-        nc.gpsimd.tensor_scalar(capped[:], exps[:], EXP_CAP, 0.0, ALU.min, ALU.max)
-        gate_pool.append(load_gates(2, "slot_g"))
+        gates = [gate_of(0)]
+        sigs = sb.tile([P, I], F32, tag="gate_pool_slot0", align_bytes=MX_ALIGN)
+        nc.scalar.activation(sigs[:], neg_scores[:], ACT.Sigmoid, bias=th_col[:])
+        floored = sb.tile([P, I], F32)
+        nc.gpsimd.tensor_scalar(floored[:], sigs[:], 1.0, SIGMOID_FLOOR, ALU.min, ALU.max)
         logs = sb.tile([P, I], F32)
-        nc.scalar.activation(logs[:], capped[:], ACT.Ln, bias=1.0)
+        nc.scalar.activation(logs[:], floored[:], ACT.Ln)
 
-        tab_codes = sb.tile([P, I], U32, align_bytes=64)
+        tab_codes = sb.tile([P, I], U32, align_bytes=MX_ALIGN)
         nc.vector.tensor_copy(tab_codes[:], tab_pool[:].indirect(token_list[:]))
 
-        gate_pool.append(load_gates(3, "slot_a"))
-        w1_q = []
-        for h in range(2):
-            w1_bf = sb.tile([P, HALF * PACK], BF16, name=f"w1_bf{h}", align_bytes=64)
-            interleave(nc.vector.tensor_copy, w1_bf[:], w1_raw[h][:])
-            w1_q.append(quantize(f"w1_{h}", w1_bf[:]))
-
-        soft = sb.tile([P, I], F32)
-        row_sum = sb.tile([P, 1], F32)
+        neg_soft = sb.tile([P, I], F32, tag="tab_pool_slot")
+        neg_sum = sb.tile([P, 1], F32)
         nc.vector.scalar_tensor_tensor(
-            soft[:], scores[:], th_col[:], logs[:], ALU.subtract, ALU.max, accum_out=row_sum[:]
+            neg_soft[:], neg_scores[:], th_col[:], logs[:], ALU.add, ALU.min, accum_out=neg_sum[:]
         )
-        z = sb.tile([P, 1], F32)
-        nc.vector.tensor_tensor(z[:], row_sum[:], reserve_col[:], ALU.add)
-        inv_z = sb.tile([P, 1], F32)
-        nc.vector.reciprocal(inv_z[:], z[:])
+        neg_z = sb.tile([P, 1], F32)
+        nc.vector.tensor_tensor(neg_z[:], neg_sum[:], reserve_col[:], ALU.subtract)
+        nc.vector.tensor_copy(out=as_words(w1_bf[1][:]), in_=as_places(w1_raw[1][:]))
+        neg_inv_z = sb.tile([P, 1], F32)
+        nc.vector.reciprocal(neg_inv_z[:], neg_z[:])
+        w1_q.append(quantize("w1_1", w1_bf[1][:]))
         w_bf = sb.tile([P, I], BF16)
         nc.vector.scalar_tensor_tensor(
             w_bf[:].rearrange("p (s t) -> p s t", t=PACK),
-            soft[:].rearrange("p (s t) -> p s t", t=PACK),
-            inv_z[:],
+            neg_soft[:].rearrange("p (s t) -> p s t", t=PACK),
+            neg_inv_z[:],
             os_rows[:].rearrange("p t s -> p s t"),
             ALU.mult,
             ALU.mult,
@@ -158,45 +168,52 @@ def tile_attend_lrgated_capped_kernel(
         w_turned = ps.tile([P, 2, Q], F32, tag="score_bank")
         for u in range(2):
             nc.tensor.transpose(w_turned[:, u, :], w_pairs[:, u : I // 2 : 2], ident[:])
-        wt_bf = sb.tile([P, Q * PACK], BF16, align_bytes=64)
-        nc.scalar.copy(
-            out=wt_bf[:].bitcast(F32).rearrange("p (q u) -> p q u", u=2),
-            in_=w_turned[:].rearrange("p u q -> p q u"),
-        )
-        wt_codes, wt_scales = quantize("wt", wt_bf[:])
 
-        result = ps.tile([P, R], F32)
-        for j in range(BLOCKS):
+        def gated_block(j):
             h, cols = j // 2, slice((j % 2) * P, (j % 2 + 1) * P)
-            gate = sb.tile([P, I], F32, name=f"gate{j}")
-            nc.scalar.activation(gate[:], gate_pool[j][:].indirect(gate_list[:]), ACT.Sigmoid)
-            zh = ps.tile([P, I], F32, bufs=3)
+            zh = ps.tile([P, I], F32, tag="product_bank", bufs=PRODUCT_BANKS)
             nc.tensor.matmul_mx(
                 out=zh[:], lhsT=w1_q[h][0][:, cols].bitcast(FP8X4), lhsT_scale=w1_q[h][1][:, cols],
                 rhs=tab_codes[:].bitcast(FP8X4), rhs_scale=tab_scale_bytes[:], start=True, stop=True,
             )
             hv = sb.tile([P, PACK, P], F32, name=f"hv{j}")
-            nc.vector.tensor_tensor(
-                hv[:].rearrange("p t (c i) -> p c t i", i=4),
-                zh[:].rearrange("p (c i t) -> p c t i", i=4, t=PACK),
-                gate[:].rearrange("p (c i t) -> p c t i", i=4, t=PACK),
-                ALU.mult,
-            )
-            h_turned = ps.tile([P, PACK, P], F32, bufs=2)
+            nc.vector.tensor_tensor(as_places(hv[:]), as_words(zh[:]), as_words(gates[j][:]), ALU.mult)
+            h_turned = ps.tile([P, PACK, P], F32, bufs=TURN_BANKS)
             for t in range(PACK):
                 nc.tensor.transpose(h_turned[:, t, :], hv[:, t, :], ident[:])
-            ht_bf = sb.tile([P, P * PACK], BF16, name=f"ht_bf{j}", align_bytes=64)
+            return h_turned
+
+        def scaled_block(j, h_turned):
+            ht_bf = sb.tile([P, P * PACK], BF16, name=f"ht_bf{j}", tag=f"gate_slot{j + 1}", align_bytes=MX_ALIGN)
             nc.vector.tensor_tensor(
                 ht_bf[:].rearrange("p (r t) -> p r t", t=PACK),
                 h_turned[:].rearrange("p t r -> p r t"),
                 vs_cols[:].unsqueeze(1).to_broadcast([P, P, PACK]),
                 ALU.mult,
             )
-            ht_codes, ht_scales = quantize(f"ht{j}", ht_bf[:])
+            return quantize(f"ht{j}", ht_bf[:])
+
+        gates.extend([gate_of(j) for j in range(1, BLOCKS)])
+        turned = [gated_block(0)]
+        ht_q = []
+        for j in range(BLOCKS):
+            if j + 1 < BLOCKS:
+                turned.append(gated_block(j + 1))
+            ht_q.append(scaled_block(j, turned[j]))
+
+        wt_bf = sb.tile([P, Q * PACK], BF16, tag=f"gate_pool_slot{BLOCKS - 2}", align_bytes=MX_ALIGN)
+        nc.scalar.copy(
+            out=wt_bf[:].bitcast(F32).rearrange("p (q u) -> p q u", u=2),
+            in_=w_turned[:].rearrange("p u q -> p q u"),
+        )
+        wt_codes, wt_scales = quantize("wt", wt_bf[:])
+        staged = sb.tile([P, R], F32, tag=f"gate_pool_slot{BLOCKS - 1}", align_bytes=MX_ALIGN)
+        for j in range(BLOCKS):
+            ht_codes, ht_scales = ht_q[j]
+            result = ps.tile([P, P], F32, tag="product_bank", bufs=PRODUCT_BANKS)
             nc.tensor.matmul_mx(
-                out=result[:, j * P : (j + 1) * P], lhsT=wt_codes[:].bitcast(FP8X4), lhsT_scale=wt_scales[:],
+                out=result[:], lhsT=wt_codes[:].bitcast(FP8X4), lhsT_scale=wt_scales[:],
                 rhs=ht_codes[:].bitcast(FP8X4), rhs_scale=ht_scales[:], start=True, stop=True,
             )
-            staged = sb.tile([P, P], F32, name=f"staged{j}")
-            nc.scalar.copy(staged[:], result[:, j * P : (j + 1) * P])
-            nc.sync.dma_start(out=out[:, j * P : (j + 1) * P], in_=staged[:])
+            nc.scalar.copy(staged[:, j * P : (j + 1) * P], result[:])
+            nc.sync.dma_start(out=out[:, j * P : (j + 1) * P], in_=staged[:, j * P : (j + 1) * P])

@@ -93,22 +93,24 @@ def tile_attend_lrgated_capped_kernel(
         gate_list = sb.tile([P, I // LIST_ROWS], U16)
         nc.sync.dma_start(gate_list[:], offs2)
         load_scale_rows(key_plane, keys_scales)
+        warm = sb.tile([P, 1], F32)
+        nc.scalar.activation(warm[:], ident[:, 0:1], ACT.Sigmoid)
         key_pool = sb.tile([P, T], U32, tag="key_pool_slot", align_bytes=MX_ALIGN)
         nc.sync.dma_start(out=key_pool[:].bitcast(I32), in_=words_of(keys_words))
         load_scale_rows(tab_plane, tab_scales)
         th_col = sb.tile([P, 1], F32)
-        nc.sync.dma_start(out=th_col[:], in_=th)
+        nc.gpsimd.dma_start(out=th_col[:], in_=th)
         gate_pool = [load_gates(0)]
         w1_raw = [load_w1_half(0)]
         tab_pool = sb.tile([P, T], U32, tag="tab_pool_slot")
         nc.sync.dma_start(out=tab_pool[:].bitcast(I32), in_=words_of(tab_words))
         w1_raw.append(load_w1_half(1))
         os_cols = sb.tile([P, PACK], F32)
-        nc.sync.dma_start(out=os_cols[:], in_=slot_factor.rearrange("o (s t) -> (o s) t", t=PACK))
+        nc.gpsimd.dma_start(out=os_cols[:], in_=slot_factor.rearrange("o (s t) -> (o s) t", t=PACK))
         reserve_col = sb.tile([P, 1], F32)
-        nc.sync.dma_start(out=reserve_col[:], in_=reserve)
+        nc.gpsimd.dma_start(out=reserve_col[:], in_=reserve)
         vs_cols = sb.tile([P, PACK], F32)
-        nc.sync.dma_start(out=vs_cols[:], in_=value_scale.rearrange("o (s t) -> (o s) t", t=PACK))
+        nc.gpsimd.dma_start(out=vs_cols[:], in_=value_scale.rearrange("o (s t) -> (o s) t", t=PACK))
         gate_pool.extend([load_gates(j) for j in range(1, BLOCKS)])
 
         q_bf = sb.tile([P, Q * PACK], BF16, align_bytes=MX_ALIGN)

@@ -78,6 +78,33 @@ def tile_attend_lrgated_capped_kernel(
             nc.scalar.activation(gate[:], gate_pool[j][:].indirect(gate_list[:]), ACT.Sigmoid)
             return gate
 
+        def spread_rows(name, cols, tag, bufs):
+            rows = ps.tile([P, PACK, P], F32, name=name, tag=tag, bufs=bufs)
+            for t in range(PACK):
+                nc.tensor.transpose(rows[:, t, :], cols[:, t : t + 1].to_broadcast([P, P]), ident[:])
+            return rows
+
+        def in_slot_order(rows):
+            return rows[:].rearrange("p t s -> p s t")
+
+        def by_place(values):
+            return values[:].rearrange("p (s t) -> p s t", t=PACK)
+
+        def turn_pairs(name, src_bf, bank_tag, bufs):
+            pairs = src_bf[:].bitcast(F32)
+            turned = ps.tile([P, 2, P], F32, name=name + "_turned", tag=bank_tag, bufs=bufs)
+            for u in range(2):
+                nc.tensor.transpose(turned[:, u, :], pairs[:, u : I // 2 : 2], ident[:])
+            return turned
+
+        def quantize_pairs(name, turned, tag):
+            grouped = sb.tile([P, P * PACK], BF16, name=name + "_bf", tag=tag, align_bytes=MX_ALIGN)
+            nc.scalar.copy(
+                out=grouped[:].bitcast(F32).rearrange("p (x u) -> p x u", u=2),
+                in_=turned[:].rearrange("p u x -> p x u"),
+            )
+            return quantize(name, grouped[:])
+
         key_plane = sb.tile([P, T], U8)
         nc.gpsimd.memset(key_plane[:, : T // 2].bitcast(I32), 0)
         nc.vector.memset(key_plane[:, T // 2 :].bitcast(I32), 0)
@@ -98,6 +125,8 @@ def tile_attend_lrgated_capped_kernel(
         key_pool = sb.tile([P, T], U32, tag="key_pool_slot", align_bytes=MX_ALIGN)
         nc.sync.dma_start(out=key_pool[:].bitcast(I32), in_=words_of(keys_words))
         load_scale_rows(tab_plane, tab_scales)
+        vs_cols = sb.tile([P, PACK], F32)
+        nc.sync.dma_start(out=vs_cols[:], in_=value_scale.rearrange("o (s t) -> (o s) t", t=PACK))
         th_col = sb.tile([P, 1], F32)
         nc.gpsimd.dma_start(out=th_col[:], in_=th)
         gate_pool = [load_gates(0)]
@@ -109,8 +138,6 @@ def tile_attend_lrgated_capped_kernel(
         nc.gpsimd.dma_start(out=os_cols[:], in_=slot_factor.rearrange("o (s t) -> (o s) t", t=PACK))
         reserve_col = sb.tile([P, 1], F32)
         nc.gpsimd.dma_start(out=reserve_col[:], in_=reserve)
-        vs_cols = sb.tile([P, PACK], F32)
-        nc.gpsimd.dma_start(out=vs_cols[:], in_=value_scale.rearrange("o (s t) -> (o s) t", t=PACK))
         gate_pool.extend([load_gates(j) for j in range(1, BLOCKS)])
 
         q_bf = sb.tile([P, Q * PACK], BF16, align_bytes=MX_ALIGN)
@@ -125,9 +152,8 @@ def tile_attend_lrgated_capped_kernel(
             out=neg_scores[:], lhsT=q_codes[:].bitcast(FP8X4), lhsT_scale=q_scales[:],
             rhs=key_codes[:].bitcast(FP8X4), rhs_scale=key_scales[:], start=True, stop=True,
         )
-        os_rows = ps.tile([P, PACK, P], F32)
-        for t in range(PACK):
-            nc.tensor.transpose(os_rows[:, t, :], os_cols[:, t : t + 1].to_broadcast([P, P]), ident[:])
+        vs_rows = spread_rows("vs_rows", vs_cols, "turn_bank", TURN_BANKS)
+        os_rows = spread_rows("os_rows", os_cols, "os_bank", 1)
 
         tab_scale_bytes = sb.tile([P, I], U8, tag="key_pool_slot", align_bytes=MX_ALIGN)
         nc.vector.tensor_copy(tab_scale_bytes[:], tab_plane[:].indirect(token_list[:]))
@@ -136,6 +162,8 @@ def tile_attend_lrgated_capped_kernel(
         w1_q = [quantize("w1_0", w1_bf[0][:])]
 
         gates = [gate_of(0)]
+        first_gate = sb.tile([P, I], F32)
+        nc.vector.tensor_tensor(by_place(first_gate), by_place(gates[0]), in_slot_order(vs_rows), ALU.mult)
         sigs = sb.tile([P, I], F32, tag="gate_pool_slot0", align_bytes=MX_ALIGN)
         nc.scalar.activation(sigs[:], neg_scores[:], ACT.Sigmoid, bias=th_col[:])
         floored = sb.tile([P, I], F32)
@@ -159,28 +187,24 @@ def tile_attend_lrgated_capped_kernel(
         w1_q.append(quantize("w1_1", w1_bf[1][:]))
         w_bf = sb.tile([P, I], BF16)
         nc.vector.scalar_tensor_tensor(
-            w_bf[:].rearrange("p (s t) -> p s t", t=PACK),
-            neg_soft[:].rearrange("p (s t) -> p s t", t=PACK),
-            neg_inv_z[:],
-            os_rows[:].rearrange("p t s -> p s t"),
-            ALU.mult,
-            ALU.mult,
+            by_place(w_bf), by_place(neg_soft), neg_inv_z[:], in_slot_order(os_rows), ALU.mult, ALU.mult
         )
-        w_pairs = w_bf[:].bitcast(F32)
-        w_turned = ps.tile([P, 2, Q], F32, tag="score_bank")
-        for u in range(2):
-            nc.tensor.transpose(w_turned[:, u, :], w_pairs[:, u : I // 2 : 2], ident[:])
+        w_turned = turn_pairs("w", w_bf, "score_bank", 1)
 
-        def gated_block(j):
+        def layer_block(j):
             h, cols = j // 2, slice((j % 2) * P, (j % 2 + 1) * P)
             zh = ps.tile([P, I], F32, tag="product_bank", bufs=PRODUCT_BANKS)
             nc.tensor.matmul_mx(
                 out=zh[:], lhsT=w1_q[h][0][:, cols].bitcast(FP8X4), lhsT_scale=w1_q[h][1][:, cols],
                 rhs=tab_codes[:].bitcast(FP8X4), rhs_scale=tab_scale_bytes[:], start=True, stop=True,
             )
+            return zh
+
+        def gated_block(j):
+            zh = layer_block(j)
             hv = sb.tile([P, PACK, P], F32, name=f"hv{j}")
             nc.vector.tensor_tensor(as_places(hv[:]), as_words(zh[:]), as_words(gates[j][:]), ALU.mult)
-            h_turned = ps.tile([P, PACK, P], F32, bufs=TURN_BANKS)
+            h_turned = ps.tile([P, PACK, P], F32, tag="turn_bank", bufs=TURN_BANKS)
             for t in range(PACK):
                 nc.tensor.transpose(h_turned[:, t, :], hv[:, t, :], ident[:])
             return h_turned
@@ -195,20 +219,18 @@ def tile_attend_lrgated_capped_kernel(
             )
             return quantize(f"ht{j}", ht_bf[:])
 
+        hw_bf = sb.tile([P, I], BF16)
+        nc.vector.tensor_tensor(hw_bf[:], layer_block(0)[:], first_gate[:], ALU.mult)
+        first_turned = turn_pairs("hw", hw_bf, "turn_bank", TURN_BANKS)
         gates.extend([gate_of(j) for j in range(1, BLOCKS)])
-        turned = [gated_block(0)]
-        ht_q = []
-        for j in range(BLOCKS):
+        turned = {1: gated_block(1)}
+        ht_q = [quantize_pairs("ht0", first_turned, "gate_pool_slot1")]
+        wt_codes, wt_scales = quantize_pairs("wt", w_turned, "gate_pool_slot2")
+        for j in range(1, BLOCKS):
             if j + 1 < BLOCKS:
-                turned.append(gated_block(j + 1))
+                turned[j + 1] = gated_block(j + 1)
             ht_q.append(scaled_block(j, turned[j]))
 
-        wt_bf = sb.tile([P, Q * PACK], BF16, tag=f"gate_pool_slot{BLOCKS - 2}", align_bytes=MX_ALIGN)
-        nc.scalar.copy(
-            out=wt_bf[:].bitcast(F32).rearrange("p (q u) -> p q u", u=2),
-            in_=w_turned[:].rearrange("p u q -> p q u"),
-        )
-        wt_codes, wt_scales = quantize("wt", wt_bf[:])
         staged = sb.tile([P, R], F32, tag=f"gate_pool_slot{BLOCKS - 1}", align_bytes=MX_ALIGN)
         for j in range(BLOCKS):
             ht_codes, ht_scales = ht_q[j]

from contextlib import ExitStack

import concourse.mybir as mybir
from concourse.masks import make_identity

F32 = mybir.dt.float32
BF16 = mybir.dt.bfloat16
I32 = mybir.dt.int32
U32 = mybir.dt.uint32
U16 = mybir.dt.uint16
U8 = mybir.dt.uint8
FP8X4 = mybir.dt.float8_e4m3fn_x4
ALU = mybir.AluOpType
ACT = mybir.ActivationFunctionType

P = 128
PACK = 4
QUADRANT = 32
SCALE_ROWS = 4
LIST_ROWS = 16
RUN = 4
MX_ALIGN = 64
D, K, R, T, I, Q, U = 512, 512, 512, 2048, 512, 128, 1024
BLOCKS = R // P
HALF = R // 2
PRODUCT_BANKS = BLOCKS
TURN_BANKS = 2
SIGMOID_FLOOR = 2.0**-24

FLOPS = 2 * (Q * I * D + R * I * K + Q * R * I)


def tile_attend_lrgated_capped_kernel(
    tc, query, keys_words, keys_scales, th, reserve, tab_words, tab_scales, w1, gtab, slot_factor, value_scale, offs2, offs, out
):
    nc = tc.nc
    with ExitStack() as ctx:
        sb = ctx.enter_context(tc.tile_pool(name="sb", bufs=1))
        ps = ctx.enter_context(tc.psum_pool(name="ps", bufs=1))


        def words_of(packed):
            return packed[0].rearrange("p n t -> p (n t)").bitcast(I32)

        def load_scale_rows(plane, rows):
            for g in range(P // QUADRANT):
                nc.sync.dma_start(
                    out=plane[QUADRANT * g : QUADRANT * g + SCALE_ROWS, :].bitcast(I32),
                    in_=rows[0, SCALE_ROWS * g : SCALE_ROWS * (g + 1), :].bitcast(I32),
                )

        def load_w1_half(h):
            raw = sb.tile([P, PACK, HALF], F32, name=f"w1_raw{h}")
            rows = w1.rearrange("(p t) r -> p t r", t=PACK)
            nc.sync.dma_start(out=raw[:], in_=rows[:, :, h * HALF : (h + 1) * HALF])
            return raw

        def load_gates(j):
            pool_j = sb.tile([P, U], F32, name=f"gate_pool{j}", tag=f"gate_pool_slot{j}", align_bytes=MX_ALIGN)
            nc.sync.dma_start(out=pool_j[:], in_=gtab[j * P : (j + 1) * P, :])
            return pool_j

        def as_words(grouped):
            return grouped.rearrange("p (c i t) -> p c t i", i=RUN, t=PACK)

        def as_places(planar):
            return planar.rearrange("p t (c i) -> p c t i", i=RUN)

        def quantize(name, src):
            width = src.shape[1] // PACK
            codes = sb.tile([P, width], U32, name=name + "_codes", align_bytes=MX_ALIGN)
            scales = sb.tile([P, width], U8, name=name + "_scales", align_bytes=MX_ALIGN)
            nc.vector.quantize_mx(out=codes[:].bitcast(FP8X4), scales=scales[:], in_=src)
            return codes, scales

        def gate_of(j):
            gate = sb.tile([P, I], F32, name=f"gate{j}", tag=f"gate_slot{j}", align_bytes=MX_ALIGN)
            nc.scalar.activation(gate[:], gate_pool[j][:].indirect(gate_list[:]), ACT.Sigmoid)
            return gate

        def spread_rows(name, cols, tag, bufs):
            rows = ps.tile([P, PACK, P], F32, name=name, tag=tag, bufs=bufs)
            for t in range(PACK):
                nc.tensor.transpose(rows[:, t, :], cols[:, t : t + 1].to_broadcast([P, P]), ident[:])
            return rows

        def in_slot_order(rows):
            return rows[:].rearrange("p t s -> p s t")

        def by_place(values):
            return values[:].rearrange("p (s t) -> p s t", t=PACK)

        def turn_pairs(name, src_bf, bank_tag, bufs):
            pairs = src_bf[:].bitcast(F32)
            turned = ps.tile([P, 2, P], F32, name=name + "_turned", tag=bank_tag, bufs=bufs)
            for u in range(2):
                nc.tensor.transpose(turned[:, u, :], pairs[:, u : I // 2 : 2], ident[:])
            return turned

        def quantize_pairs(name, turned, tag):
            grouped = sb.tile([P, P * PACK], BF16, name=name + "_bf", tag=tag, align_bytes=MX_ALIGN)
            nc.scalar.copy(
                out=grouped[:].bitcast(F32).rearrange("p (x u) -> p x u", u=2),
                in_=turned[:].rearrange("p u x -> p x u"),
            )
            return quantize(name, grouped[:])

        key_plane = sb.tile([P, T], U8)
        nc.gpsimd.memset(key_plane[:, : T // 2].bitcast(I32), 0)
        nc.vector.memset(key_plane[:, T // 2 :].bitcast(I32), 0)
        tab_plane = sb.tile([P, T], U8)
        nc.vector.memset(tab_plane[:].bitcast(I32), 0)
        ident = sb.tile([P, P], F32)
        make_identity(nc, ident[:])

        token_list = sb.tile([P, I // LIST_ROWS], U16)
        nc.sync.dma_start(token_list[:], offs)
        q_raw = sb.tile([P, PACK, Q], F32)
        nc.sync.dma_start(out=q_raw[:], in_=query.rearrange("(p t) q -> p t q", t=PACK))
        gate_list = sb.tile([P, I // LIST_ROWS], U16)
        nc.sync.dma_start(gate_list[:], offs2)
        load_scale_rows(key_plane, keys_scales)
        warm = sb.tile([P, 1], F32)
        nc.scalar.activation(warm[:], ident[:, 0:1], ACT.Sigmoid)
        key_pool = sb.tile([P, T], U32, tag="key_pool_slot", align_bytes=MX_ALIGN)
        nc.sync.dma_start(out=key_pool[:].bitcast(I32), in_=words_of(keys_words))
        load_scale_rows(tab_plane, tab_scales)
        vs_cols = sb.tile([P, PACK], F32)
        nc.sync.dma_start(out=vs_cols[:], in_=value_scale.rearrange("o (s t) -> (o s) t", t=PACK))
        th_col = sb.tile([P, 1], F32)
        nc.gpsimd.dma_start(out=th_col[:], in_=th)
        gate_pool = [load_gates(0)]
        w1_raw = [load_w1_half(0)]
        tab_pool = sb.tile([P, T], U32, tag="tab_pool_slot")
        nc.sync.dma_start(out=tab_pool[:].bitcast(I32), in_=words_of(tab_words))
        w1_raw.append(load_w1_half(1))
        os_cols = sb.tile([P, PACK], F32)
        nc.gpsimd.dma_start(out=os_cols[:], in_=slot_factor.rearrange("o (s t) -> (o s) t", t=PACK))
        reserve_col = sb.tile([P, 1], F32)
        nc.gpsimd.dma_start(out=reserve_col[:], in_=reserve)
        gate_pool.extend([load_gates(j) for j in range(1, BLOCKS)])

        q_bf = sb.tile([P, Q * PACK], BF16, align_bytes=MX_ALIGN)
        nc.vector.tensor_scalar(as_words(q_bf[:]), as_places(q_raw[:]), -1.0, None, ALU.mult)
        key_scales = sb.tile([P, I], U8, align_bytes=MX_ALIGN)
        nc.vector.tensor_copy(key_scales[:], key_plane[:].indirect(token_list[:]))
        q_codes, q_scales = quantize("q", q_bf[:])
        key_codes = sb.tile([P, I], U32, align_bytes=MX_ALIGN)
        nc.vector.tensor_copy(key_codes[:], key_pool[:].indirect(token_list[:]))
        neg_scores = ps.tile([P, I], F32, tag="score_bank")
        nc.tensor.matmul_mx(
            out=neg_scores[:], lhsT=q_codes[:].bitcast(FP8X4), lhsT_scale=q_scales[:],
            rhs=key_codes[:].bitcast(FP8X4), rhs_scale=key_scales[:], start=True, stop=True,
        )
        vs_rows = spread_rows("vs_rows", vs_cols, "turn_bank", TURN_BANKS)
        os_rows = spread_rows("os_rows", os_cols, "os_bank", 1)

        tab_scale_bytes = sb.tile([P, I], U8, tag="key_pool_slot", align_bytes=MX_ALIGN)
        nc.vector.tensor_copy(tab_scale_bytes[:], tab_plane[:].indirect(token_list[:]))
        w1_bf = [sb.tile([P, HALF * PACK], BF16, name=f"w1_bf{h}", align_bytes=MX_ALIGN) for h in range(2)]
        nc.vector.tensor_copy(out=as_words(w1_bf[0][:]), in_=as_places(w1_raw[0][:]))
        w1_q = [quantize("w1_0", w1_bf[0][:])]

        gates = [gate_of(0)]
        first_gate = sb.tile([P, I], F32)
        nc.vector.tensor_tensor(by_place(first_gate), by_place(gates[0]), in_slot_order(vs_rows), ALU.mult)
        sigs = sb.tile([P, I], F32, tag="gate_pool_slot0", align_bytes=MX_ALIGN)
        nc.scalar.activation(sigs[:], neg_scores[:], ACT.Sigmoid, bias=th_col[:])
        floored = sb.tile([P, I], F32)
        nc.gpsimd.tensor_scalar(floored[:], sigs[:], 1.0, SIGMOID_FLOOR, ALU.min, ALU.max)
        logs = sb.tile([P, I], F32)
        nc.scalar.activation(logs[:], floored[:], ACT.Ln)

        tab_codes = sb.tile([P, I], U32, align_bytes=MX_ALIGN)
        nc.vector.tensor_copy(tab_codes[:], tab_pool[:].indirect(token_list[:]))

        neg_soft = sb.tile([P, I], F32, tag="tab_pool_slot")
        neg_sum = sb.tile([P, 1], F32)
        nc.vector.scalar_tensor_tensor(
            neg_soft[:], neg_scores[:], th_col[:], logs[:], ALU.add, ALU.min, accum_out=neg_sum[:]
        )
        neg_z = sb.tile([P, 1], F32)
        nc.vector.tensor_tensor(neg_z[:], neg_sum[:], reserve_col[:], ALU.subtract)
        nc.vector.tensor_copy(out=as_words(w1_bf[1][:]), in_=as_places(w1_raw[1][:]))
        neg_inv_z = sb.tile([P, 1], F32)
        nc.vector.reciprocal(neg_inv_z[:], neg_z[:])
        w1_q.append(quantize("w1_1", w1_bf[1][:]))
        w_bf = sb.tile([P, I], BF16)
        nc.vector.scalar_tensor_tensor(
            by_place(w_bf), by_place(neg_soft), neg_inv_z[:], in_slot_order(os_rows), ALU.mult, ALU.mult
        )
        w_turned = turn_pairs("w", w_bf, "score_bank", 1)

        def layer_block(j):
            h, cols = j // 2, slice((j % 2) * P, (j % 2 + 1) * P)
            zh = ps.tile([P, I], F32, tag="product_bank", bufs=PRODUCT_BANKS)
            nc.tensor.matmul_mx(
                out=zh[:], lhsT=w1_q[h][0][:, cols].bitcast(FP8X4), lhsT_scale=w1_q[h][1][:, cols],
                rhs=tab_codes[:].bitcast(FP8X4), rhs_scale=tab_scale_bytes[:], start=True, stop=True,
            )
            return zh

        def gated_block(j):
            zh = layer_block(j)
            hv = sb.tile([P, PACK, P], F32, name=f"hv{j}")
            nc.vector.tensor_tensor(as_places(hv[:]), as_words(zh[:]), as_words(gates[j][:]), ALU.mult)
            h_turned = ps.tile([P, PACK, P], F32, tag="turn_bank", bufs=TURN_BANKS)
            for t in range(PACK):
                nc.tensor.transpose(h_turned[:, t, :], hv[:, t, :], ident[:])
            return h_turned

        def scaled_block(j, h_turned):
            ht_bf = sb.tile([P, P * PACK], BF16, name=f"ht_bf{j}", tag=f"gate_slot{j + 1}", align_bytes=MX_ALIGN)
            nc.vector.tensor_tensor(
                ht_bf[:].rearrange("p (r t) -> p r t", t=PACK),
                h_turned[:].rearrange("p t r -> p r t"),
                vs_cols[:].unsqueeze(1).to_broadcast([P, P, PACK]),
                ALU.mult,
            )
            return quantize(f"ht{j}", ht_bf[:])

        hw_bf = sb.tile([P, I], BF16)
        nc.vector.tensor_tensor(hw_bf[:], layer_block(0)[:], first_gate[:], ALU.mult)
        first_turned = turn_pairs("hw", hw_bf, "turn_bank", TURN_BANKS)
        gates.extend([gate_of(j) for j in range(1, BLOCKS)])
        turned = {1: gated_block(1)}
        ht_q = [quantize_pairs("ht0", first_turned, "gate_pool_slot1")]
        wt_codes, wt_scales = quantize_pairs("wt", w_turned, "gate_pool_slot2")
        for j in range(1, BLOCKS):
            if j + 1 < BLOCKS:
                turned[j + 1] = gated_block(j + 1)
            ht_q.append(scaled_block(j, turned[j]))

        staged = sb.tile([P, R], F32, tag=f"gate_pool_slot{BLOCKS - 1}", align_bytes=MX_ALIGN)
        for j in range(BLOCKS):
            ht_codes, ht_scales = ht_q[j]
            result = ps.tile([P, P], F32, tag="product_bank", bufs=PRODUCT_BANKS)
            nc.tensor.matmul_mx(
                out=result[:], lhsT=wt_codes[:].bitcast(FP8X4), lhsT_scale=wt_scales[:],
                rhs=ht_codes[:].bitcast(FP8X4), rhs_scale=ht_scales[:], start=True, stop=True,
            )
            nc.scalar.copy(staged[:, j * P : (j + 1) * P], result[:])
            nc.sync.dma_start(out=out[:, j * P : (j + 1) * P], in_=staged[:, j * P : (j + 1) * P])
